import numpy as np
import ml_dtypes


def mxq(x, axis, fmt="e4m3"):
    dtype, down = {"e4m3": (ml_dtypes.float8_e4m3fn, 7), "e5m2": (ml_dtypes.float8_e5m2, 14)}[fmt]
    v = np.moveaxis(np.asarray(x, np.float32).astype(ml_dtypes.bfloat16).astype(np.float64), axis, -1)
    blocks = v.reshape(v.shape[:-1] + (-1, 32))
    amax = np.abs(blocks).max(-1, keepdims=True)
    byte = np.maximum(np.where(amax > 0, np.frexp(amax)[1] - 1 + 127, 0) - down, 1)
    scale = np.exp2(byte - 127.0)
    codes = (blocks / scale).astype(np.float32).astype(dtype).astype(np.float64)
    return np.moveaxis((codes * scale).reshape(v.shape), -1, axis)


WIDE = False


def mx_kscale(k):
    if not WIDE:
        return np.ones(k)
    levels = np.array([10, -10, 5, -5, 0])
    if k % 512:
        return np.exp2(np.random.permutation(np.resize(levels, k // 32))).repeat(32)
    a = np.empty((k // 512, 16))
    for p in range(k // 512):
        a[p, :8] = np.random.permutation(np.resize(levels, 8))
        for g in range(8):
            far = levels[np.abs(levels - a[p, g]) >= 10]
            a[p, g + 8] = far[np.random.randint(len(far))]
    return np.exp2(a.ravel()).repeat(32)


def f64(x):
    return np.asarray(x).astype(np.float64)


def striped(idx):
    return np.tile(np.asarray(idx).reshape(-1, 16).T, (8, 1)).astype(np.uint16)


def unstriped(offs):
    return offs[:16].T.reshape(-1).astype(np.int64)


E2M1 = np.array([0.0, 0.5, 1.0, 1.5, 2.0, 3.0, 4.0, 6.0, -0.0, -0.5, -1.0, -1.5, -2.0, -3.0, -4.0, -6.0])


def pack_weight(w, fmt):
    k, n = w.shape
    w = f64(np.asarray(w, np.float32).astype(ml_dtypes.bfloat16)).reshape(k // 32, 32, n)
    amax = np.abs(w).max(1)
    if fmt == "e4m3":
        byte = np.frexp(amax)[1] - 1 + 127 - 7
    else:
        mant, ex = np.frexp(amax / 6.0)
        byte = np.where(mant > 0.5, ex, ex - 1) + 127
    byte = np.clip(np.where(amax > 0, byte, 1), 1, 254)
    scaled = (w * np.exp2(127.0 - byte)[:, None, :]).reshape(k, n).astype(np.float32)
    by_word = np.ascontiguousarray(scaled.reshape(k // 512, 128, 4, n).transpose(0, 1, 3, 2))
    if fmt == "e4m3":
        words = by_word.astype(ml_dtypes.float8_e4m3fn).view(np.uint8)
    else:
        c = by_word.astype(ml_dtypes.float4_e2m1fn).view(np.uint8) & 0xF
        words = (c[..., 0::2] | (c[..., 1::2] << 4)).reshape(k // 512, 128, 2 * n)
    return np.ascontiguousarray(words), np.ascontiguousarray(byte.astype(np.uint8).reshape(k // 512, 16, n))


def unpack_weight(words, scales, fmt):
    g, _, n = scales.shape
    words = np.ascontiguousarray(words).reshape(g, 128, n, -1)
    if fmt == "e4m3":
        vals = words.view(ml_dtypes.float8_e4m3fn).astype(np.float64)
    else:
        nib = np.empty((g, 128, n, 4), np.uint8)
        nib[..., 0::2] = words & 0xF
        nib[..., 1::2] = words >> 4
        vals = E2M1[nib]
    vals = vals * np.repeat(np.exp2(scales.astype(np.float64) - 127.0), 8, axis=1)[..., None]
    return vals.transpose(0, 1, 3, 2).reshape(g * 512, n)


def bf(x):
    return np.asarray(x, np.float32).astype(ml_dtypes.bfloat16)


def planes(Y):
    r, m = Y.shape
    b = f64(bf(Y)).reshape(r // 32, 32, m)
    amax = np.abs(b).max(1)
    byte = np.clip(np.where(amax > 0, np.frexp(amax)[1] - 1 + 127 - 7, 1), 1, 254)
    codes = (b * np.exp2(127.0 - byte)[:, None, :]).reshape(r, m).astype(np.float32).astype(ml_dtypes.float8_e4m3fn).view(np.uint8)
    words = codes.reshape(r // 512, 128, 4, m).transpose(0, 1, 3, 2)
    return np.ascontiguousarray(words), np.ascontiguousarray(byte.astype(np.uint8).reshape(r // 512, 16, m))


D, E, T, I, Q = 512, 512, 2048, 512, 256


def setup_inputs():
    n = np.random.standard_normal
    idx = np.random.permutation(T)[:I]
    fd = mx_kscale(D)
    fi = mx_kscale(I)
    ti = np.ones(T)
    ti[idx] = fi
    keysp = pack_weight(n((D, T)) / fd[:, None], "e2m1")
    return {
        "query": (n((D, Q)) * 1.0 / np.sqrt(D) * fd[:, None]).astype(np.float32),
        "keys_words": keysp[0],
        "keys_scales": keysp[1],
        "aim": (np.random.uniform(0.5, 2.0, (Q, 1))).astype(np.float32),
        "soft": (np.random.uniform(0.5, 2.0, (Q, 1))).astype(np.float32),
        "os": (np.random.uniform(4.0, 16.0, (1, I)) * fi).astype(np.float32),
        "vals": (n((E, T)) / ti).astype(np.float32),
        "offs": striped(idx),
    }


def reference(query, keys_words, keys_scales, aim, soft, os, vals, offs):
    idx = unstriped(offs)
    keysu = unpack_weight(keys_words, keys_scales, "e2m1")
    queryq = mxq(f64(query), 0, "e4m3")
    keysidxg = keysu[:, idx]
    a = queryq.T @ keysidxg
    p = 1.0 / (np.square(f64(aim) - a) + f64(soft))
    z = np.sum(p, axis=1, keepdims=True)
    w = p / z
    wo1 = w * f64(os)
    wt1 = wo1.T
    vt1 = f64(vals)[:, idx].T
    vt1q = mxq(vt1, 0, "e4m3")
    wt1q = mxq(wt1, 0, "e4m3")
    o = vt1q.T @ wt1q
    words, scales = planes(o)
    return o, words, scales

@@ -1,0 +1,185 @@
+from contextlib import ExitStack
+
+import concourse.mybir as mybir
+from concourse.masks import make_identity
+
+D, E, T, I, Q = 512, 512, 2048, 512, 256
+FLOPS = 2 * D * Q * I + 2 * I * E * Q
+
+F32 = mybir.dt.float32
+BF16 = mybir.dt.bfloat16
+I32 = mybir.dt.int32
+U32 = mybir.dt.uint32
+U16 = mybir.dt.uint16
+U8 = mybir.dt.uint8
+FP8X4 = mybir.dt.float8_e4m3fn_x4
+FP4X4 = mybir.dt.float4_e2m1fn_x4
+ACT = mybir.ActivationFunctionType
+ALU = mybir.AluOpType
+
+P = 128
+PACK = 4
+HALVES = Q // P
+
+
+def tile_attend_nearpoint_pl_kernel(tc, query, keys_words, keys_scales, aim, soft, slot_factor, vals, offs, out_0, out_1, out_2):
+    nc = tc.nc
+    with ExitStack() as ctx:
+        sb = ctx.enter_context(tc.tile_pool(name="sb", bufs=1))
+        ps = ctx.enter_context(tc.psum_pool(name="ps", bufs=1))
+
+        offsets = sb.tile([P, I // 16], U16, name="offsets")
+        nc.sync.dma_start(offsets[:], offs)
+
+        key_scale_pool = sb.tile([P, T], U8, name="key_scale_pool", align_bytes=64)
+        nc.vector.memset(key_scale_pool[:].bitcast(I32), 0)
+        key_pool = sb.tile([P, T], U16, name="key_pool", align_bytes=64)
+        nc.sync.dma_start(key_pool[:].bitcast(I32), keys_words[0].bitcast(I32))
+        for quad in range(4):
+            nc.scalar.dma_start(
+                key_scale_pool[32 * quad : 32 * quad + 4, :].bitcast(I32),
+                keys_scales[0, 4 * quad : 4 * quad + 4, :].bitcast(I32),
+            )
+
+        aims = sb.tile([P, HALVES], F32, name="aims")
+        nc.sync.dma_start(aims[:], aim.rearrange("(p h) one -> p (h one)", h=HALVES))
+        softs = sb.tile([P, HALVES], F32, name="softs")
+        nc.sync.dma_start(softs[:], soft.rearrange("(p h) one -> p (h one)", h=HALVES))
+        factors = sb.tile([P, PACK], F32, name="factors")
+        nc.sync.dma_start(factors[:], slot_factor.rearrange("one (s j) -> (one s) j", j=PACK))
+        query_rows = sb.tile([P, PACK, Q], F32, name="query_rows")
+        nc.sync.dma_start(query_rows[:], query.rearrange("(p j) q -> p j q", j=PACK))
+        ident = sb.tile([P, P], F32, name="ident")
+        make_identity(nc, ident[:])
+
+        val_planes = vals.rearrange("(p t) c -> t p c", t=PACK)
+        val_pools = []
+        for t in range(PACK):
+            val_pool = sb.tile([P, T], F32, name="val_pool%d" % t)
+            nc.sync.dma_start(val_pool[:], val_planes[t])
+            val_pools.append(val_pool)
+
+        warm_in = sb.tile([P, 1], F32, name="warm_in")
+        nc.vector.memset(warm_in[:], 1.0)
+        warm_out = sb.tile([P, 1], F32, name="warm_out")
+        nc.scalar.activation(warm_out[:], warm_in[:], ACT.Abs_reciprocal_sqrt)
+
+        keys = sb.tile([P, I], U16, name="keys", align_bytes=64)
+        nc.vector.tensor_copy(keys[:], key_pool[:].indirect(offsets[:]))
+        key_scales = sb.tile([P, I], U8, name="key_scales", align_bytes=64)
+        nc.vector.tensor_copy(key_scales[:], key_scale_pool[:].indirect(offsets[:]))
+
+        query_bf = sb.tile([P, HALVES, P, PACK], BF16, name="query_bf", align_bytes=64)
+        nc.scalar.copy(query_bf[:], query_rows[:].rearrange("p j (m h) -> p h m j", h=HALVES))
+        query_codes = sb.tile([P, Q], U32, name="query_codes", align_bytes=64)
+        query_scales = sb.tile([P, Q], U8, name="query_scales", align_bytes=64)
+        nc.vector.quantize_mx(query_codes[:].bitcast(FP8X4), query_scales[:], query_bf[:].rearrange("p h m j -> p (h m j)"))
+
+        factor_rows = ps.tile([P, PACK, P], F32, name="factor_rows")
+        for j in range(PACK):
+            nc.tensor.transpose(factor_rows[:, j, :], factors[:, j : j + 1].to_broadcast([P, P]), ident[:])
+
+        weights_turned = ps.tile([P, HALVES, 2, P], F32, name="weights_turned")
+        for h in range(HALVES):
+            cols = slice(h * P, (h + 1) * P)
+            scores = ps.tile([P, I], F32, name="scores%d" % h)
+            nc.tensor.matmul_mx(
+                scores[:],
+                lhsT=query_codes[:, cols].bitcast(FP8X4),
+                lhsT_scale=query_scales[:, cols],
+                rhs=keys[:].bitcast(FP4X4),
+                rhs_scale=key_scales[:],
+                start=True,
+                stop=True,
+            )
+            gap = sb.tile([P, I], F32, name="gap%d" % h)
+            nc.scalar.activation(gap[:], scores[:], ACT.Square, bias=aims[:, h : h + 1], scale=-1.0)
+            root = sb.tile([P, I], F32, name="root%d" % h)
+            nc.scalar.activation(root[:], gap[:], ACT.Abs_reciprocal_sqrt, bias=softs[:, h : h + 1])
+            part = sb.tile([P, I], F32, name="part%d" % h)
+            total = sb.tile([P, 1], F32, name="total%d" % h)
+            nc.scalar.activation(part[:], root[:], ACT.Square, accum_out=total[:])
+            inverse = sb.tile([P, 1], F32, name="inverse%d" % h)
+            nc.vector.reciprocal(inverse[:], total[:])
+            weights = sb.tile([P, I], BF16, name="weights%d" % h, align_bytes=64)
+            nc.vector.scalar_tensor_tensor(
+                weights[:].rearrange("m (s j) -> m s j", j=PACK),
+                part[:].rearrange("m (s j) -> m s j", j=PACK),
+                inverse[:],
+                factor_rows[:].rearrange("m j s -> m s j"),
+                ALU.mult,
+                ALU.mult,
+            )
+            pairs = weights[:].bitcast(F32)
+            for u in range(2):
+                nc.tensor.transpose(weights_turned[:, h, u, :], pairs[:, u : I // 2 : 2], ident[:])
+        weights_bf = sb.tile([P, Q * PACK], BF16, name="weights_bf", align_bytes=64)
+        nc.scalar.copy(
+            weights_bf[:].bitcast(F32).rearrange("s (m h u) -> s m h u", h=HALVES, u=2),
+            weights_turned[:].rearrange("s h u m -> s m h u"),
+        )
+        weight_codes = sb.tile([P, Q], U32, name="weight_codes", align_bytes=64)
+        weight_scales = sb.tile([P, Q], U8, name="weight_scales", align_bytes=64)
+        nc.vector.quantize_mx(weight_codes[:].bitcast(FP8X4), weight_scales[:], weights_bf[:])
+
+        sums = [ps.tile([P, PACK, P], F32, name="sums%d" % g) for g in range(HALVES)]
+        result = sb.tile([P, PACK, Q], F32, name="result")
+        out_rows = out_0.rearrange("(p t) q -> p t q", t=PACK)
+        for t in range(PACK):
+            picked = sb.tile([P, I], BF16, name="picked%d" % t, align_bytes=64)
+            nc.vector.tensor_copy(picked[:], val_pools[t][:].indirect(offsets[:]))
+            turned = ps.tile([P, 2, P], F32, name="turned%d" % (t % 2))
+            pairs = picked[:].bitcast(F32)
+            for u in range(2):
+                nc.tensor.transpose(turned[:, u, :], pairs[:, u : I // 2 : 2], ident[:])
+            val_bf = sb.tile([P, P * PACK], BF16, name="val_bf%d" % t, align_bytes=64)
+            nc.scalar.copy(
+                val_bf[:].bitcast(F32).rearrange("s (m u) -> s m u", u=2),
+                turned[:].rearrange("s u m -> s m u"),
+            )
+            val_codes = sb.tile([P, P], U32, name="val_codes%d" % t, align_bytes=64)
+            val_scales = sb.tile([P, P], U8, name="val_scales%d" % t, align_bytes=64)
+            nc.vector.quantize_mx(val_codes[:].bitcast(FP8X4), val_scales[:], val_bf[:])
+            for g in range(HALVES):
+                cols = slice(g * P, (g + 1) * P)
+                nc.tensor.matmul_mx(
+                    sums[g][:, t, :],
+                    lhsT=val_codes[:].bitcast(FP8X4),
+                    lhsT_scale=val_scales[:],
+                    rhs=weight_codes[:, cols].bitcast(FP8X4),
+                    rhs_scale=weight_scales[:, cols],
+                    start=True,
+                    stop=True,
+                )
+            if t == PACK - 2:
+                for g in range(HALVES):
+                    nc.scalar.copy(result[:, : PACK - 1, g * P : (g + 1) * P], sums[g][:, : PACK - 1, :])
+                nc.sync.dma_start(out_rows[:, : PACK - 1, :], result[:, : PACK - 1, :])
+
+        result_codes = sb.tile([P, Q], U32, name="result_codes", align_bytes=64)
+        result_scales = sb.tile([P, Q], U8, name="result_scales", align_bytes=64)
+        result_bf = []
+        for g in range(HALVES):
+            rounded = sb.tile([P, P, PACK], BF16, name="rounded%d" % g, align_bytes=64)
+            if g == 0:
+                nc.scalar.copy(rounded[:], sums[g][:].rearrange("p t m -> p m t"))
+            else:
+                nc.vector.tensor_copy(rounded[:], sums[g][:].rearrange("p t m -> p m t"))
+            result_bf.append(rounded)
+        for g in range(HALVES):
+            nc.scalar.copy(result[:, PACK - 1, g * P : (g + 1) * P], sums[g][:, PACK - 1, :])
+        nc.sync.dma_start(out_rows[:, PACK - 1, :], result[:, PACK - 1, :])
+        for g in range(HALVES):
+            cols = slice(g * P, (g + 1) * P)
+            nc.vector.quantize_mx(
+                result_codes[:, cols].bitcast(FP8X4),
+                result_scales[:, cols],
+                result_bf[g][:].rearrange("p m t -> p (m t)"),
+            )
+        nc.sync.dma_start(out_1[0].rearrange("p c r -> p (c r)").bitcast(I32), result_codes[:].bitcast(I32))
+        for quad in range(4):
+            queue = nc.scalar if quad % 2 else nc.sync
+            queue.dma_start(
+                out_2[0, 4 * quad : 4 * quad + 4, :].bitcast(I32),
+                result_scales[32 * quad : 32 * quad + 4, :].bitcast(I32),
+            )

@@ -31,31 +31,33 @@ def tile_attend_nearpoint_pl_kernel(tc, query, keys_words, keys_scales, aim, sof
         offsets = sb.tile([P, I // 16], U16, name="offsets")
         nc.sync.dma_start(offsets[:], offs)
 
+        aims = sb.tile([P, HALVES], F32, name="aims")
+        with nc.allow_non_contiguous_dma(reason="one value for each half of the query rows"):
+            nc.sync.dma_start(aims[:], aim.rearrange("(h p) one -> p (h one)", h=HALVES))
         key_scale_pool = sb.tile([P, T], U8, name="key_scale_pool", align_bytes=64)
-        nc.vector.memset(key_scale_pool[:].bitcast(I32), 0)
-        key_pool = sb.tile([P, T], U16, name="key_pool", align_bytes=64)
-        nc.sync.dma_start(key_pool[:].bitcast(I32), keys_words[0].bitcast(I32))
+        nc.vector.memset(key_scale_pool[:, : T // 2].bitcast(I32), 0)
+        nc.gpsimd.memset(key_scale_pool[:, T // 2 :].bitcast(I32), 0)
         for quad in range(4):
-            nc.scalar.dma_start(
+            nc.sync.dma_start(
                 key_scale_pool[32 * quad : 32 * quad + 4, :].bitcast(I32),
                 keys_scales[0, 4 * quad : 4 * quad + 4, :].bitcast(I32),
             )
-
-        aims = sb.tile([P, HALVES], F32, name="aims")
-        nc.sync.dma_start(aims[:], aim.rearrange("(p h) one -> p (h one)", h=HALVES))
-        softs = sb.tile([P, HALVES], F32, name="softs")
-        nc.sync.dma_start(softs[:], soft.rearrange("(p h) one -> p (h one)", h=HALVES))
-        factors = sb.tile([P, PACK], F32, name="factors")
-        nc.sync.dma_start(factors[:], slot_factor.rearrange("one (s j) -> (one s) j", j=PACK))
+        key_pool = sb.tile([P, T], U16, name="key_pool", align_bytes=64)
+        nc.sync.dma_start(key_pool[:].bitcast(I32), keys_words[0].bitcast(I32))
         query_rows = sb.tile([P, PACK, Q], F32, name="query_rows")
         nc.sync.dma_start(query_rows[:], query.rearrange("(p j) q -> p j q", j=PACK))
+        softs = sb.tile([P, HALVES], F32, name="softs")
+        with nc.allow_non_contiguous_dma(reason="one value for each half of the query rows"):
+            nc.sync.dma_start(softs[:], soft.rearrange("(h p) one -> p (h one)", h=HALVES))
+        factors = sb.tile([P, PACK], F32, name="factors")
+        nc.sync.dma_start(factors[:], slot_factor.rearrange("one (s j) -> (one s) j", j=PACK))
         ident = sb.tile([P, P], F32, name="ident")
         make_identity(nc, ident[:])
 
         val_planes = vals.rearrange("(p t) c -> t p c", t=PACK)
         val_pools = []
         for t in range(PACK):
-            val_pool = sb.tile([P, T], F32, name="val_pool%d" % t)
+            val_pool = sb.tile([P, T], F32, name="val_pool%d" % t, tag="plane%d" % t, align_bytes=64)
             nc.sync.dma_start(val_pool[:], val_planes[t])
             val_pools.append(val_pool)
 
@@ -64,97 +66,123 @@ def tile_attend_nearpoint_pl_kernel(tc, query, keys_words, keys_scales, aim, sof
         warm_out = sb.tile([P, 1], F32, name="warm_out")
         nc.scalar.activation(warm_out[:], warm_in[:], ACT.Abs_reciprocal_sqrt)
 
-        keys = sb.tile([P, I], U16, name="keys", align_bytes=64)
-        nc.vector.tensor_copy(keys[:], key_pool[:].indirect(offsets[:]))
         key_scales = sb.tile([P, I], U8, name="key_scales", align_bytes=64)
         nc.vector.tensor_copy(key_scales[:], key_scale_pool[:].indirect(offsets[:]))
+        keys = sb.tile([P, I], U16, name="keys", align_bytes=64)
+        nc.vector.tensor_copy(keys[:], key_pool[:].indirect(offsets[:]))
 
-        query_bf = sb.tile([P, HALVES, P, PACK], BF16, name="query_bf", align_bytes=64)
-        nc.scalar.copy(query_bf[:], query_rows[:].rearrange("p j (m h) -> p h m j", h=HALVES))
-        query_codes = sb.tile([P, Q], U32, name="query_codes", align_bytes=64)
-        query_scales = sb.tile([P, Q], U8, name="query_scales", align_bytes=64)
-        nc.vector.quantize_mx(query_codes[:].bitcast(FP8X4), query_scales[:], query_bf[:].rearrange("p h m j -> p (h m j)"))
+        query_codes, query_scales = [], []
+        for h in range(HALVES):
+            query_bf = sb.tile([P, P, PACK], BF16, name="query_bf%d" % h, align_bytes=64)
+            half = query_rows[:, :, h * P : (h + 1) * P].rearrange("p j m -> p m j")
+            if h == 0:
+                nc.scalar.copy(query_bf[:], half)
+            else:
+                nc.vector.tensor_copy(query_bf[:], half)
+            codes = sb.tile([P, P], U32, name="query_codes%d" % h, align_bytes=64)
+            scales = sb.tile([P, P], U8, name="query_scales%d" % h, align_bytes=64)
+            nc.vector.quantize_mx(codes[:].bitcast(FP8X4), scales[:], query_bf[:].rearrange("p m j -> p (m j)"))
+            query_codes.append(codes)
+            query_scales.append(scales)
 
         factor_rows = ps.tile([P, PACK, P], F32, name="factor_rows")
         for j in range(PACK):
             nc.tensor.transpose(factor_rows[:, j, :], factors[:, j : j + 1].to_broadcast([P, P]), ident[:])
 
-        weights_turned = ps.tile([P, HALVES, 2, P], F32, name="weights_turned")
+        def turn(rows, dest, bank):
+            turned = ps.tile([P, 2, P], F32, name=bank)
+            pairs = rows[:].bitcast(F32)
+            for u in range(2):
+                nc.tensor.transpose(turned[:, u, :], pairs[:, u : I // 2 : 2], ident[:])
+            nc.scalar.copy(
+                dest.bitcast(F32).rearrange("s (m u) -> s m u", u=2),
+                turned[:].rearrange("s u m -> s m u"),
+            )
+
+        def gather_and_turn(t, dest):
+            picked = sb.tile([P, I], BF16, name="picked%d" % t, tag="part1" if t == 2 else "picked%d" % t, align_bytes=64)
+            nc.vector.tensor_copy(picked[:], val_pools[t][:].indirect(offsets[:]))
+            turn(picked, dest, "turned%d" % (t % 2))
+
+        parts, totals = [], []
         for h in range(HALVES):
-            cols = slice(h * P, (h + 1) * P)
             scores = ps.tile([P, I], F32, name="scores%d" % h)
             nc.tensor.matmul_mx(
                 scores[:],
-                lhsT=query_codes[:, cols].bitcast(FP8X4),
-                lhsT_scale=query_scales[:, cols],
+                lhsT=query_codes[h][:].bitcast(FP8X4),
+                lhsT_scale=query_scales[h][:],
                 rhs=keys[:].bitcast(FP4X4),
                 rhs_scale=key_scales[:],
                 start=True,
                 stop=True,
             )
-            gap = sb.tile([P, I], F32, name="gap%d" % h)
+            gap = sb.tile([P, I], F32, name="gap%d" % h, tag="gap")
             nc.scalar.activation(gap[:], scores[:], ACT.Square, bias=aims[:, h : h + 1], scale=-1.0)
-            root = sb.tile([P, I], F32, name="root%d" % h)
+            root = sb.tile([P, I], F32, name="root%d" % h, tag="root%d" % h, align_bytes=64)
             nc.scalar.activation(root[:], gap[:], ACT.Abs_reciprocal_sqrt, bias=softs[:, h : h + 1])
-            part = sb.tile([P, I], F32, name="part%d" % h)
+            part = sb.tile([P, I], F32, name="part%d" % h, tag="part%d" % h, align_bytes=64)
             total = sb.tile([P, 1], F32, name="total%d" % h)
             nc.scalar.activation(part[:], root[:], ACT.Square, accum_out=total[:])
-            inverse = sb.tile([P, 1], F32, name="inverse%d" % h)
-            nc.vector.reciprocal(inverse[:], total[:])
+            totals.append(total)
+            parts.append(part)
+
+        early_bf = sb.tile([P, 2 * I + Q * PACK], BF16, name="early_bf", tag="root1", align_bytes=64)
+        for h in range(HALVES):
+            gather_and_turn(h, early_bf[:, h * I : (h + 1) * I])
+            inverse = sb.tile([P, 1], F32, name="inverse%d" % h, tag="plane%d" % h, align_bytes=64)
+            nc.vector.reciprocal(inverse[:], totals[h][:])
             weights = sb.tile([P, I], BF16, name="weights%d" % h, align_bytes=64)
             nc.vector.scalar_tensor_tensor(
                 weights[:].rearrange("m (s j) -> m s j", j=PACK),
-                part[:].rearrange("m (s j) -> m s j", j=PACK),
+                parts[h][:].rearrange("m (s j) -> m s j", j=PACK),
                 inverse[:],
                 factor_rows[:].rearrange("m j s -> m s j"),
                 ALU.mult,
                 ALU.mult,
             )
-            pairs = weights[:].bitcast(F32)
-            for u in range(2):
-                nc.tensor.transpose(weights_turned[:, h, u, :], pairs[:, u : I // 2 : 2], ident[:])
-        weights_bf = sb.tile([P, Q * PACK], BF16, name="weights_bf", align_bytes=64)
-        nc.scalar.copy(
-            weights_bf[:].bitcast(F32).rearrange("s (m h u) -> s m h u", h=HALVES, u=2),
-            weights_turned[:].rearrange("s h u m -> s m h u"),
-        )
-        weight_codes = sb.tile([P, Q], U32, name="weight_codes", align_bytes=64)
-        weight_scales = sb.tile([P, Q], U8, name="weight_scales", align_bytes=64)
-        nc.vector.quantize_mx(weight_codes[:].bitcast(FP8X4), weight_scales[:], weights_bf[:])
+            turn(weights, early_bf[:, (2 + h) * I : (3 + h) * I], "turned2")
+
+        late_bf = [sb.tile([P, I], BF16, name="late_bf%d" % t, align_bytes=64) for t in range(2)]
+        gather_and_turn(2, late_bf[0][:])
+        early_codes = sb.tile([P, 2 * P + Q], U32, name="early_codes", tag="plane2", align_bytes=64)
+        early_scales = sb.tile([P, 2 * P + Q], U8, name="early_scales", align_bytes=64)
+        nc.vector.quantize_mx(early_codes[:].bitcast(FP8X4), early_scales[:], early_bf[:])
 
         sums = [ps.tile([P, PACK, P], F32, name="sums%d" % g) for g in range(HALVES)]
         result = sb.tile([P, PACK, Q], F32, name="result")
         out_rows = out_0.rearrange("(p t) q -> p t q", t=PACK)
-        for t in range(PACK):
-            picked = sb.tile([P, I], BF16, name="picked%d" % t, align_bytes=64)
-            nc.vector.tensor_copy(picked[:], val_pools[t][:].indirect(offsets[:]))
-            turned = ps.tile([P, 2, P], F32, name="turned%d" % (t % 2))
-            pairs = picked[:].bitcast(F32)
-            for u in range(2):
-                nc.tensor.transpose(turned[:, u, :], pairs[:, u : I // 2 : 2], ident[:])
-            val_bf = sb.tile([P, P * PACK], BF16, name="val_bf%d" % t, align_bytes=64)
-            nc.scalar.copy(
-                val_bf[:].bitcast(F32).rearrange("s (m u) -> s m u", u=2),
-                turned[:].rearrange("s u m -> s m u"),
-            )
-            val_codes = sb.tile([P, P], U32, name="val_codes%d" % t, align_bytes=64)
-            val_scales = sb.tile([P, P], U8, name="val_scales%d" % t, align_bytes=64)
-            nc.vector.quantize_mx(val_codes[:].bitcast(FP8X4), val_scales[:], val_bf[:])
+
+        def multiply(t, codes, scales):
             for g in range(HALVES):
-                cols = slice(g * P, (g + 1) * P)
+                cols = slice((2 + g) * P, (3 + g) * P)
                 nc.tensor.matmul_mx(
                     sums[g][:, t, :],
-                    lhsT=val_codes[:].bitcast(FP8X4),
-                    lhsT_scale=val_scales[:],
-                    rhs=weight_codes[:, cols].bitcast(FP8X4),
-                    rhs_scale=weight_scales[:, cols],
+                    lhsT=codes.bitcast(FP8X4),
+                    lhsT_scale=scales,
+                    rhs=early_codes[:, cols].bitcast(FP8X4),
+                    rhs_scale=early_scales[:, cols],
                     start=True,
                     stop=True,
                 )
-            if t == PACK - 2:
-                for g in range(HALVES):
-                    nc.scalar.copy(result[:, : PACK - 1, g * P : (g + 1) * P], sums[g][:, : PACK - 1, :])
-                nc.sync.dma_start(out_rows[:, : PACK - 1, :], result[:, : PACK - 1, :])
+
+        def store(planes):
+            for g in range(HALVES):
+                nc.scalar.copy(result[:, planes, g * P : (g + 1) * P], sums[g][:, planes, :])
+            nc.sync.dma_start(out_rows[:, planes, :], result[:, planes, :])
+
+        for t in range(2):
+            multiply(t, early_codes[:, t * P : (t + 1) * P], early_scales[:, t * P : (t + 1) * P])
+        store(slice(0, 2))
+        gather_and_turn(3, late_bf[1][:])
+        codes2 = sb.tile([P, P], U32, name="codes2", tag="plane3", align_bytes=64)
+        scales2 = sb.tile([P, P], U8, name="scales2", align_bytes=64)
+        nc.vector.quantize_mx(codes2[:].bitcast(FP8X4), scales2[:], late_bf[0][:])
+        multiply(2, codes2[:], scales2[:])
+        store(slice(2, 3))
+        codes3 = sb.tile([P, P], U32, name="codes3", align_bytes=64)
+        scales3 = sb.tile([P, P], U8, name="scales3", align_bytes=64)
+        nc.vector.quantize_mx(codes3[:].bitcast(FP8X4), scales3[:], late_bf[1][:])
+        multiply(3, codes3[:], scales3[:])
 
         result_codes = sb.tile([P, Q], U32, name="result_codes", align_bytes=64)
         result_scales = sb.tile([P, Q], U8, name="result_scales", align_bytes=64)
@@ -166,9 +194,7 @@ def tile_attend_nearpoint_pl_kernel(tc, query, keys_words, keys_scales, aim, sof
             else:
                 nc.vector.tensor_copy(rounded[:], sums[g][:].rearrange("p t m -> p m t"))
             result_bf.append(rounded)
-        for g in range(HALVES):
-            nc.scalar.copy(result[:, PACK - 1, g * P : (g + 1) * P], sums[g][:, PACK - 1, :])
-        nc.sync.dma_start(out_rows[:, PACK - 1, :], result[:, PACK - 1, :])
+        store(slice(3, 4))
         for g in range(HALVES):
             cols = slice(g * P, (g + 1) * P)
             nc.vector.quantize_mx(

@@ -31,9 +31,8 @@ def tile_attend_nearpoint_pl_kernel(tc, query, keys_words, keys_scales, aim, sof
         offsets = sb.tile([P, I // 16], U16, name="offsets")
         nc.sync.dma_start(offsets[:], offs)
 
-        aims = sb.tile([P, HALVES], F32, name="aims")
-        with nc.allow_non_contiguous_dma(reason="one value for each half of the query rows"):
-            nc.sync.dma_start(aims[:], aim.rearrange("(h p) one -> p (h one)", h=HALVES))
+        key_pool = sb.tile([P, T], U16, name="key_pool", align_bytes=64)
+        nc.sync.dma_start(key_pool[:].bitcast(I32), keys_words[0].bitcast(I32))
         key_scale_pool = sb.tile([P, T], U8, name="key_scale_pool", align_bytes=64)
         nc.vector.memset(key_scale_pool[:, : T // 2].bitcast(I32), 0)
         nc.gpsimd.memset(key_scale_pool[:, T // 2 :].bitcast(I32), 0)
@@ -42,52 +41,46 @@ def tile_attend_nearpoint_pl_kernel(tc, query, keys_words, keys_scales, aim, sof
                 key_scale_pool[32 * quad : 32 * quad + 4, :].bitcast(I32),
                 keys_scales[0, 4 * quad : 4 * quad + 4, :].bitcast(I32),
             )
-        key_pool = sb.tile([P, T], U16, name="key_pool", align_bytes=64)
-        nc.sync.dma_start(key_pool[:].bitcast(I32), keys_words[0].bitcast(I32))
         query_rows = sb.tile([P, PACK, Q], F32, name="query_rows")
         nc.sync.dma_start(query_rows[:], query.rearrange("(p j) q -> p j q", j=PACK))
+        aims = sb.tile([P, HALVES], F32, name="aims")
+        with nc.allow_non_contiguous_dma(reason="one value for each half of the query rows"):
+            nc.sync.dma_start(aims[:], aim.rearrange("(h p) one -> p (h one)", h=HALVES))
+        ident = sb.tile([P, P], F32, name="ident")
+        make_identity(nc, ident[:])
+
+        val_planes = vals.rearrange("(p t) c -> t p c", t=PACK)
+        val_pools = [
+            sb.tile([P, T], F32, name="val_pool%d" % t, tag="plane%d" % t, align_bytes=64) for t in range(PACK)
+        ]
+        nc.sync.dma_start(val_pools[0][:], val_planes[0])
         softs = sb.tile([P, HALVES], F32, name="softs")
         with nc.allow_non_contiguous_dma(reason="one value for each half of the query rows"):
             nc.sync.dma_start(softs[:], soft.rearrange("(h p) one -> p (h one)", h=HALVES))
         factors = sb.tile([P, PACK], F32, name="factors")
         nc.sync.dma_start(factors[:], slot_factor.rearrange("one (s j) -> (one s) j", j=PACK))
-        ident = sb.tile([P, P], F32, name="ident")
-        make_identity(nc, ident[:])
-
-        val_planes = vals.rearrange("(p t) c -> t p c", t=PACK)
-        val_pools = []
-        for t in range(PACK):
-            val_pool = sb.tile([P, T], F32, name="val_pool%d" % t, tag="plane%d" % t, align_bytes=64)
-            nc.sync.dma_start(val_pool[:], val_planes[t])
-            val_pools.append(val_pool)
+        for t in range(1, PACK):
+            nc.sync.dma_start(val_pools[t][:], val_planes[t])
 
         warm_in = sb.tile([P, 1], F32, name="warm_in")
         nc.vector.memset(warm_in[:], 1.0)
         warm_out = sb.tile([P, 1], F32, name="warm_out")
         nc.scalar.activation(warm_out[:], warm_in[:], ACT.Abs_reciprocal_sqrt)
 
-        key_scales = sb.tile([P, I], U8, name="key_scales", align_bytes=64)
-        nc.vector.tensor_copy(key_scales[:], key_scale_pool[:].indirect(offsets[:]))
         keys = sb.tile([P, I], U16, name="keys", align_bytes=64)
         nc.vector.tensor_copy(keys[:], key_pool[:].indirect(offsets[:]))
+        key_scales = sb.tile([P, I], U8, name="key_scales", align_bytes=64)
+        nc.vector.tensor_copy(key_scales[:], key_scale_pool[:].indirect(offsets[:]))
 
         query_codes, query_scales = [], []
         for h in range(HALVES):
             query_bf = sb.tile([P, P, PACK], BF16, name="query_bf%d" % h, align_bytes=64)
-            half = query_rows[:, :, h * P : (h + 1) * P].rearrange("p j m -> p m j")
-            if h == 0:
-                nc.scalar.copy(query_bf[:], half)
-            else:
-                nc.vector.tensor_copy(query_bf[:], half)
+            nc.scalar.copy(query_bf[:], query_rows[:, :, h * P : (h + 1) * P].rearrange("p j m -> p m j"))
             codes = sb.tile([P, P], U32, name="query_codes%d" % h, align_bytes=64)
             scales = sb.tile([P, P], U8, name="query_scales%d" % h, align_bytes=64)
             nc.vector.quantize_mx(codes[:].bitcast(FP8X4), scales[:], query_bf[:].rearrange("p m j -> p (m j)"))
             query_codes.append(codes)
             query_scales.append(scales)
-
-        factor_rows = ps.tile([P, PACK, P], F32, name="factor_rows")
-        for j in range(PACK):
-            nc.tensor.transpose(factor_rows[:, j, :], factors[:, j : j + 1].to_broadcast([P, P]), ident[:])
 
         def turn(rows, dest, bank):
             turned = ps.tile([P, 2, P], F32, name=bank)
@@ -102,9 +95,10 @@ def tile_attend_nearpoint_pl_kernel(tc, query, keys_words, keys_scales, aim, sof
         def gather_and_turn(t, dest):
             picked = sb.tile([P, I], BF16, name="picked%d" % t, tag="part1" if t == 2 else "picked%d" % t, align_bytes=64)
             nc.vector.tensor_copy(picked[:], val_pools[t][:].indirect(offsets[:]))
-            turn(picked, dest, "turned%d" % (t % 2))
+            turn(picked, dest, ("turned0", "turned1", "scores1", "turned0")[t])
 
-        parts, totals = [], []
+        parts = []
+        totals = sb.tile([P, HALVES], F32, name="totals")
         for h in range(HALVES):
             scores = ps.tile([P, I], F32, name="scores%d" % h)
             nc.tensor.matmul_mx(
@@ -116,91 +110,84 @@ def tile_attend_nearpoint_pl_kernel(tc, query, keys_words, keys_scales, aim, sof
                 start=True,
                 stop=True,
             )
-            gap = sb.tile([P, I], F32, name="gap%d" % h, tag="gap")
+            gap = sb.tile([P, I], F32, name="gap%d" % h)
             nc.scalar.activation(gap[:], scores[:], ACT.Square, bias=aims[:, h : h + 1], scale=-1.0)
             root = sb.tile([P, I], F32, name="root%d" % h, tag="root%d" % h, align_bytes=64)
             nc.scalar.activation(root[:], gap[:], ACT.Abs_reciprocal_sqrt, bias=softs[:, h : h + 1])
             part = sb.tile([P, I], F32, name="part%d" % h, tag="part%d" % h, align_bytes=64)
-            total = sb.tile([P, 1], F32, name="total%d" % h)
-            nc.scalar.activation(part[:], root[:], ACT.Square, accum_out=total[:])
-            totals.append(total)
+            nc.scalar.activation(part[:], root[:], ACT.Square, accum_out=totals[:, h : h + 1])
             parts.append(part)
 
+        factor_rows = ps.tile([P, PACK, P], F32, name="factor_rows")
+        for j in range(PACK):
+            nc.tensor.transpose(factor_rows[:, j, :], factors[:, j : j + 1].to_broadcast([P, P]), ident[:])
+
         early_bf = sb.tile([P, 2 * I + Q * PACK], BF16, name="early_bf", tag="root1", align_bytes=64)
+        for t in range(2):
+            gather_and_turn(t, early_bf[:, t * I : (t + 1) * I])
+        inverse = sb.tile([P, HALVES], F32, name="inverse", tag="plane1", align_bytes=64)
+        nc.vector.reciprocal(inverse[:], totals[:])
         for h in range(HALVES):
-            gather_and_turn(h, early_bf[:, h * I : (h + 1) * I])
-            inverse = sb.tile([P, 1], F32, name="inverse%d" % h, tag="plane%d" % h, align_bytes=64)
-            nc.vector.reciprocal(inverse[:], totals[h][:])
             weights = sb.tile([P, I], BF16, name="weights%d" % h, align_bytes=64)
             nc.vector.scalar_tensor_tensor(
                 weights[:].rearrange("m (s j) -> m s j", j=PACK),
                 parts[h][:].rearrange("m (s j) -> m s j", j=PACK),
-                inverse[:],
+                inverse[:, h : h + 1],
                 factor_rows[:].rearrange("m j s -> m s j"),
                 ALU.mult,
                 ALU.mult,
             )
-            turn(weights, early_bf[:, (2 + h) * I : (3 + h) * I], "turned2")
+            turn(weights, early_bf[:, (2 + h) * I : (3 + h) * I], "scores%d" % h)
 
         late_bf = [sb.tile([P, I], BF16, name="late_bf%d" % t, align_bytes=64) for t in range(2)]
         gather_and_turn(2, late_bf[0][:])
-        early_codes = sb.tile([P, 2 * P + Q], U32, name="early_codes", tag="plane2", align_bytes=64)
-        early_scales = sb.tile([P, 2 * P + Q], U8, name="early_scales", align_bytes=64)
-        nc.vector.quantize_mx(early_codes[:].bitcast(FP8X4), early_scales[:], early_bf[:])
+        gather_and_turn(3, late_bf[1][:])
+        early_codes = sb.tile([P, 3 * P + Q], U32, name="early_codes", tag="plane3", align_bytes=64)
+        early_scales = sb.tile([P, 3 * P + Q], U8, name="early_scales", align_bytes=64)
+        nc.vector.quantize_mx(early_codes[:, : 4 * P].bitcast(FP8X4), early_scales[:, : 4 * P], early_bf[:])
+        nc.vector.quantize_mx(early_codes[:, 4 * P :].bitcast(FP8X4), early_scales[:, 4 * P :], late_bf[0][:])
+        last_codes = sb.tile([P, P], U32, name="last_codes", align_bytes=64)
+        last_scales = sb.tile([P, P], U8, name="last_scales", align_bytes=64)
+        plane_cols = [slice(0, P), slice(P, 2 * P), slice(4 * P, 5 * P)]
+        plane_codes = [early_codes[:, cols] for cols in plane_cols] + [last_codes[:]]
+        plane_scales = [early_scales[:, cols] for cols in plane_cols] + [last_scales[:]]
 
-        sums = [ps.tile([P, PACK, P], F32, name="sums%d" % g) for g in range(HALVES)]
         result = sb.tile([P, PACK, Q], F32, name="result")
         out_rows = out_0.rearrange("(p t) q -> p t q", t=PACK)
 
-        def multiply(t, codes, scales):
-            for g in range(HALVES):
-                cols = slice((2 + g) * P, (3 + g) * P)
+        def multiply(bank, planes):
+            sums = ps.tile([P, len(planes), Q], F32, name=bank)
+            for place, t in enumerate(planes):
                 nc.tensor.matmul_mx(
-                    sums[g][:, t, :],
-                    lhsT=codes.bitcast(FP8X4),
-                    lhsT_scale=scales,
-                    rhs=early_codes[:, cols].bitcast(FP8X4),
-                    rhs_scale=early_scales[:, cols],
+                    sums[:, place, :],
+                    lhsT=plane_codes[t].bitcast(FP8X4),
+                    lhsT_scale=plane_scales[t],
+                    rhs=early_codes[:, 2 * P : 4 * P].bitcast(FP8X4),
+                    rhs_scale=early_scales[:, 2 * P : 4 * P],
                     start=True,
                     stop=True,
                 )
+            return sums
 
-        def store(planes):
-            for g in range(HALVES):
-                nc.scalar.copy(result[:, planes, g * P : (g + 1) * P], sums[g][:, planes, :])
-            nc.sync.dma_start(out_rows[:, planes, :], result[:, planes, :])
-
-        for t in range(2):
-            multiply(t, early_codes[:, t * P : (t + 1) * P], early_scales[:, t * P : (t + 1) * P])
-        store(slice(0, 2))
-        gather_and_turn(3, late_bf[1][:])
-        codes2 = sb.tile([P, P], U32, name="codes2", tag="plane3", align_bytes=64)
-        scales2 = sb.tile([P, P], U8, name="scales2", align_bytes=64)
-        nc.vector.quantize_mx(codes2[:].bitcast(FP8X4), scales2[:], late_bf[0][:])
-        multiply(2, codes2[:], scales2[:])
-        store(slice(2, 3))
-        codes3 = sb.tile([P, P], U32, name="codes3", align_bytes=64)
-        scales3 = sb.tile([P, P], U8, name="scales3", align_bytes=64)
-        nc.vector.quantize_mx(codes3[:].bitcast(FP8X4), scales3[:], late_bf[1][:])
-        multiply(3, codes3[:], scales3[:])
+        nc.scalar.copy(result[:, 0:2, :], multiply("sums01", (0, 1))[:])
+        nc.sync.dma_start(out_rows[:, 0:2, :], result[:, 0:2, :])
+        sums2 = multiply("sums2", (2,))
+        nc.vector.quantize_mx(last_codes[:].bitcast(FP8X4), last_scales[:], late_bf[1][:])
+        nc.vector.tensor_copy(result[:, 2:3, :], sums2[:])
+        nc.vector.tensor_copy(result[:, 3:4, :], multiply("sums3", (3,))[:])
+        nc.sync.dma_start(out_rows[:, 2:4, :], result[:, 2:4, :])
 
         result_codes = sb.tile([P, Q], U32, name="result_codes", align_bytes=64)
         result_scales = sb.tile([P, Q], U8, name="result_scales", align_bytes=64)
-        result_bf = []
-        for g in range(HALVES):
-            rounded = sb.tile([P, P, PACK], BF16, name="rounded%d" % g, align_bytes=64)
-            if g == 0:
-                nc.scalar.copy(rounded[:], sums[g][:].rearrange("p t m -> p m t"))
-            else:
-                nc.vector.tensor_copy(rounded[:], sums[g][:].rearrange("p t m -> p m t"))
-            result_bf.append(rounded)
-        store(slice(3, 4))
-        for g in range(HALVES):
+        rounded = [sb.tile([P, P, PACK], BF16, name="rounded%d" % g, align_bytes=64) for g in range(HALVES)]
+        nc.scalar.copy(rounded[0][:], result[:, :, :P].rearrange("p t m -> p m t"))
+        nc.vector.tensor_copy(rounded[1][:], result[:, :, P:].rearrange("p t m -> p m t"))
+        for g in (1, 0):
             cols = slice(g * P, (g + 1) * P)
             nc.vector.quantize_mx(
                 result_codes[:, cols].bitcast(FP8X4),
                 result_scales[:, cols],
-                result_bf[g][:].rearrange("p m t -> p (m t)"),
+                rounded[g][:].rearrange("p m t -> p (m t)"),
             )
         nc.sync.dma_start(out_1[0].rearrange("p c r -> p (c r)").bitcast(I32), result_codes[:].bitcast(I32))
         for quad in range(4):

@@ -44,8 +44,7 @@ def tile_attend_nearpoint_pl_kernel(tc, query, keys_words, keys_scales, aim, sof
         query_rows = sb.tile([P, PACK, Q], F32, name="query_rows")
         nc.sync.dma_start(query_rows[:], query.rearrange("(p j) q -> p j q", j=PACK))
         aims = sb.tile([P, HALVES], F32, name="aims")
-        with nc.allow_non_contiguous_dma(reason="one value for each half of the query rows"):
-            nc.sync.dma_start(aims[:], aim.rearrange("(h p) one -> p (h one)", h=HALVES))
+        nc.sync.dma_start(aims[:], aim.rearrange("(p h) one -> p (h one)", h=HALVES))
         ident = sb.tile([P, P], F32, name="ident")
         make_identity(nc, ident[:])
 
@@ -55,8 +54,7 @@ def tile_attend_nearpoint_pl_kernel(tc, query, keys_words, keys_scales, aim, sof
         ]
         nc.sync.dma_start(val_pools[0][:], val_planes[0])
         softs = sb.tile([P, HALVES], F32, name="softs")
-        with nc.allow_non_contiguous_dma(reason="one value for each half of the query rows"):
-            nc.sync.dma_start(softs[:], soft.rearrange("(h p) one -> p (h one)", h=HALVES))
+        nc.sync.dma_start(softs[:], soft.rearrange("(p h) one -> p (h one)", h=HALVES))
         factors = sb.tile([P, PACK], F32, name="factors")
         nc.sync.dma_start(factors[:], slot_factor.rearrange("one (s j) -> (one s) j", j=PACK))
         for t in range(1, PACK):
@@ -75,7 +73,10 @@ def tile_attend_nearpoint_pl_kernel(tc, query, keys_words, keys_scales, aim, sof
         query_codes, query_scales = [], []
         for h in range(HALVES):
             query_bf = sb.tile([P, P, PACK], BF16, name="query_bf%d" % h, align_bytes=64)
-            nc.scalar.copy(query_bf[:], query_rows[:, :, h * P : (h + 1) * P].rearrange("p j m -> p m j"))
+            nc.scalar.copy(
+                query_bf[:].rearrange("p (c i) j -> p c j i", i=4),
+                query_rows[:].rearrange("p j (c i h) -> p h c j i", i=4, h=HALVES)[:, h],
+            )
             codes = sb.tile([P, P], U32, name="query_codes%d" % h, align_bytes=64)
             scales = sb.tile([P, P], U8, name="query_scales%d" % h, align_bytes=64)
             nc.vector.quantize_mx(codes[:].bitcast(FP8X4), scales[:], query_bf[:].rearrange("p m j -> p (m j)"))
@@ -167,21 +168,25 @@ def tile_attend_nearpoint_pl_kernel(tc, query, keys_words, keys_scales, aim, sof
                     start=True,
                     stop=True,
                 )
-            return sums
+            return sums[:].rearrange("p t (h m) -> p t m h", h=HALVES)
 
-        nc.scalar.copy(result[:, 0:2, :], multiply("sums01", (0, 1))[:])
+        dealt = result[:].rearrange("p t (m h) -> p t m h", h=HALVES)
+        nc.scalar.copy(dealt[:, 0:2], multiply("sums01", (0, 1)))
         nc.sync.dma_start(out_rows[:, 0:2, :], result[:, 0:2, :])
         sums2 = multiply("sums2", (2,))
         nc.vector.quantize_mx(last_codes[:].bitcast(FP8X4), last_scales[:], late_bf[1][:])
-        nc.vector.tensor_copy(result[:, 2:3, :], sums2[:])
-        nc.vector.tensor_copy(result[:, 3:4, :], multiply("sums3", (3,))[:])
+        nc.vector.tensor_copy(dealt[:, 2:3], sums2)
+        nc.vector.tensor_copy(dealt[:, 3:4], multiply("sums3", (3,)))
         nc.sync.dma_start(out_rows[:, 2:4, :], result[:, 2:4, :])
 
         result_codes = sb.tile([P, Q], U32, name="result_codes", align_bytes=64)
         result_scales = sb.tile([P, Q], U8, name="result_scales", align_bytes=64)
         rounded = [sb.tile([P, P, PACK], BF16, name="rounded%d" % g, align_bytes=64) for g in range(HALVES)]
-        nc.scalar.copy(rounded[0][:], result[:, :, :P].rearrange("p t m -> p m t"))
-        nc.vector.tensor_copy(rounded[1][:], result[:, :, P:].rearrange("p t m -> p m t"))
+        for g, copy in enumerate((nc.scalar.copy, nc.vector.tensor_copy)):
+            copy(
+                rounded[g][:].rearrange("p (c i) t -> p c t i", i=4),
+                result[:, :, g * P : (g + 1) * P].rearrange("p t (c i) -> p c t i", i=4),
+            )
         for g in (1, 0):
             cols = slice(g * P, (g + 1) * P)
             nc.vector.quantize_mx(

from contextlib import ExitStack

import concourse.mybir as mybir
from concourse.masks import make_identity

D, E, T, I, Q = 512, 512, 2048, 512, 256
FLOPS = 2 * D * Q * I + 2 * I * E * Q

F32 = mybir.dt.float32
BF16 = mybir.dt.bfloat16
I32 = mybir.dt.int32
U32 = mybir.dt.uint32
U16 = mybir.dt.uint16
U8 = mybir.dt.uint8
FP8X4 = mybir.dt.float8_e4m3fn_x4
FP4X4 = mybir.dt.float4_e2m1fn_x4
ACT = mybir.ActivationFunctionType
ALU = mybir.AluOpType

P = 128
PACK = 4
HALVES = Q // P


def tile_attend_nearpoint_pl_kernel(tc, query, keys_words, keys_scales, aim, soft, slot_factor, vals, offs, out_0, out_1, out_2):
    nc = tc.nc
    with ExitStack() as ctx:
        sb = ctx.enter_context(tc.tile_pool(name="sb", bufs=1))
        ps = ctx.enter_context(tc.psum_pool(name="ps", bufs=1))

        offsets = sb.tile([P, I // 16], U16, name="offsets")
        nc.sync.dma_start(offsets[:], offs)

        key_pool = sb.tile([P, T], U16, name="key_pool", align_bytes=64)
        nc.sync.dma_start(key_pool[:].bitcast(I32), keys_words[0].bitcast(I32))
        key_scale_pool = sb.tile([P, T], U8, name="key_scale_pool", align_bytes=64)
        nc.vector.memset(key_scale_pool[:, : T // 2].bitcast(I32), 0)
        nc.gpsimd.memset(key_scale_pool[:, T // 2 :].bitcast(I32), 0)
        for quad in range(4):
            nc.sync.dma_start(
                key_scale_pool[32 * quad : 32 * quad + 4, :].bitcast(I32),
                keys_scales[0, 4 * quad : 4 * quad + 4, :].bitcast(I32),
            )
        query_rows = sb.tile([P, PACK, Q], F32, name="query_rows")
        nc.sync.dma_start(query_rows[:], query.rearrange("(p j) q -> p j q", j=PACK))
        aims = sb.tile([P, HALVES], F32, name="aims")
        nc.sync.dma_start(aims[:], aim.rearrange("(p h) one -> p (h one)", h=HALVES))
        ident = sb.tile([P, P], F32, name="ident")
        make_identity(nc, ident[:])

        val_planes = vals.rearrange("(p t) c -> t p c", t=PACK)
        val_pools = [
            sb.tile([P, T], F32, name="val_pool%d" % t, tag="plane%d" % t, align_bytes=64) for t in range(PACK)
        ]
        nc.sync.dma_start(val_pools[0][:], val_planes[0])
        softs = sb.tile([P, HALVES], F32, name="softs")
        nc.sync.dma_start(softs[:], soft.rearrange("(p h) one -> p (h one)", h=HALVES))
        factors = sb.tile([P, PACK], F32, name="factors")
        nc.sync.dma_start(factors[:], slot_factor.rearrange("one (s j) -> (one s) j", j=PACK))
        for t in range(1, PACK):
            nc.sync.dma_start(val_pools[t][:], val_planes[t])

        warm_in = sb.tile([P, 1], F32, name="warm_in")
        nc.vector.memset(warm_in[:], 1.0)
        warm_out = sb.tile([P, 1], F32, name="warm_out")
        nc.scalar.activation(warm_out[:], warm_in[:], ACT.Abs_reciprocal_sqrt)

        keys = sb.tile([P, I], U16, name="keys", align_bytes=64)
        nc.vector.tensor_copy(keys[:], key_pool[:].indirect(offsets[:]))
        key_scales = sb.tile([P, I], U8, name="key_scales", align_bytes=64)
        nc.vector.tensor_copy(key_scales[:], key_scale_pool[:].indirect(offsets[:]))

        query_codes, query_scales = [], []
        for h in range(HALVES):
            query_bf = sb.tile([P, P, PACK], BF16, name="query_bf%d" % h, align_bytes=64)
            nc.scalar.copy(
                query_bf[:].rearrange("p (c i) j -> p c j i", i=4),
                query_rows[:].rearrange("p j (c i h) -> p h c j i", i=4, h=HALVES)[:, h],
            )
            codes = sb.tile([P, P], U32, name="query_codes%d" % h, align_bytes=64)
            scales = sb.tile([P, P], U8, name="query_scales%d" % h, align_bytes=64)
            nc.vector.quantize_mx(codes[:].bitcast(FP8X4), scales[:], query_bf[:].rearrange("p m j -> p (m j)"))
            query_codes.append(codes)
            query_scales.append(scales)

        def turn(rows, dest, bank):
            turned = ps.tile([P, 2, P], F32, name=bank)
            pairs = rows[:].bitcast(F32)
            for u in range(2):
                nc.tensor.transpose(turned[:, u, :], pairs[:, u : I // 2 : 2], ident[:])
            nc.scalar.copy(
                dest.bitcast(F32).rearrange("s (m u) -> s m u", u=2),
                turned[:].rearrange("s u m -> s m u"),
            )

        def gather_and_turn(t, dest):
            picked = sb.tile([P, I], BF16, name="picked%d" % t, tag="part1" if t == 2 else "picked%d" % t, align_bytes=64)
            nc.vector.tensor_copy(picked[:], val_pools[t][:].indirect(offsets[:]))
            turn(picked, dest, ("turned0", "turned1", "scores1", "turned0")[t])

        parts = []
        totals = sb.tile([P, HALVES], F32, name="totals")
        for h in range(HALVES):
            scores = ps.tile([P, I], F32, name="scores%d" % h)
            nc.tensor.matmul_mx(
                scores[:],
                lhsT=query_codes[h][:].bitcast(FP8X4),
                lhsT_scale=query_scales[h][:],
                rhs=keys[:].bitcast(FP4X4),
                rhs_scale=key_scales[:],
                start=True,
                stop=True,
            )
            gap = sb.tile([P, I], F32, name="gap%d" % h)
            nc.scalar.activation(gap[:], scores[:], ACT.Square, bias=aims[:, h : h + 1], scale=-1.0)
            root = sb.tile([P, I], F32, name="root%d" % h, tag="root%d" % h, align_bytes=64)
            nc.scalar.activation(root[:], gap[:], ACT.Abs_reciprocal_sqrt, bias=softs[:, h : h + 1])
            part = sb.tile([P, I], F32, name="part%d" % h, tag="part%d" % h, align_bytes=64)
            nc.scalar.activation(part[:], root[:], ACT.Square, accum_out=totals[:, h : h + 1])
            parts.append(part)

        factor_rows = ps.tile([P, PACK, P], F32, name="factor_rows")
        for j in range(PACK):
            nc.tensor.transpose(factor_rows[:, j, :], factors[:, j : j + 1].to_broadcast([P, P]), ident[:])

        early_bf = sb.tile([P, 2 * I + Q * PACK], BF16, name="early_bf", tag="root1", align_bytes=64)
        for t in range(2):
            gather_and_turn(t, early_bf[:, t * I : (t + 1) * I])
        inverse = sb.tile([P, HALVES], F32, name="inverse", tag="plane1", align_bytes=64)
        nc.vector.reciprocal(inverse[:], totals[:])
        for h in range(HALVES):
            weights = sb.tile([P, I], BF16, name="weights%d" % h, align_bytes=64)
            nc.vector.scalar_tensor_tensor(
                weights[:].rearrange("m (s j) -> m s j", j=PACK),
                parts[h][:].rearrange("m (s j) -> m s j", j=PACK),
                inverse[:, h : h + 1],
                factor_rows[:].rearrange("m j s -> m s j"),
                ALU.mult,
                ALU.mult,
            )
            turn(weights, early_bf[:, (2 + h) * I : (3 + h) * I], "scores%d" % h)

        late_bf = [sb.tile([P, I], BF16, name="late_bf%d" % t, align_bytes=64) for t in range(2)]
        gather_and_turn(2, late_bf[0][:])
        gather_and_turn(3, late_bf[1][:])
        early_codes = sb.tile([P, 3 * P + Q], U32, name="early_codes", tag="plane3", align_bytes=64)
        early_scales = sb.tile([P, 3 * P + Q], U8, name="early_scales", align_bytes=64)
        nc.vector.quantize_mx(early_codes[:, : 4 * P].bitcast(FP8X4), early_scales[:, : 4 * P], early_bf[:])
        nc.vector.quantize_mx(early_codes[:, 4 * P :].bitcast(FP8X4), early_scales[:, 4 * P :], late_bf[0][:])
        last_codes = sb.tile([P, P], U32, name="last_codes", align_bytes=64)
        last_scales = sb.tile([P, P], U8, name="last_scales", align_bytes=64)
        plane_cols = [slice(0, P), slice(P, 2 * P), slice(4 * P, 5 * P)]
        plane_codes = [early_codes[:, cols] for cols in plane_cols] + [last_codes[:]]
        plane_scales = [early_scales[:, cols] for cols in plane_cols] + [last_scales[:]]

        result = sb.tile([P, PACK, Q], F32, name="result")
        out_rows = out_0.rearrange("(p t) q -> p t q", t=PACK)

        def multiply(bank, planes):
            sums = ps.tile([P, len(planes), Q], F32, name=bank)
            for place, t in enumerate(planes):
                nc.tensor.matmul_mx(
                    sums[:, place, :],
                    lhsT=plane_codes[t].bitcast(FP8X4),
                    lhsT_scale=plane_scales[t],
                    rhs=early_codes[:, 2 * P : 4 * P].bitcast(FP8X4),
                    rhs_scale=early_scales[:, 2 * P : 4 * P],
                    start=True,
                    stop=True,
                )
            return sums[:].rearrange("p t (h m) -> p t m h", h=HALVES)

        dealt = result[:].rearrange("p t (m h) -> p t m h", h=HALVES)
        nc.scalar.copy(dealt[:, 0:2], multiply("sums01", (0, 1)))
        nc.sync.dma_start(out_rows[:, 0:2, :], result[:, 0:2, :])
        sums2 = multiply("sums2", (2,))
        nc.vector.quantize_mx(last_codes[:].bitcast(FP8X4), last_scales[:], late_bf[1][:])
        nc.vector.tensor_copy(dealt[:, 2:3], sums2)
        nc.vector.tensor_copy(dealt[:, 3:4], multiply("sums3", (3,)))
        nc.sync.dma_start(out_rows[:, 2:4, :], result[:, 2:4, :])

        result_codes = sb.tile([P, Q], U32, name="result_codes", align_bytes=64)
        result_scales = sb.tile([P, Q], U8, name="result_scales", align_bytes=64)
        rounded = [sb.tile([P, P, PACK], BF16, name="rounded%d" % g, align_bytes=64) for g in range(HALVES)]
        for g, copy in enumerate((nc.scalar.copy, nc.vector.tensor_copy)):
            copy(
                rounded[g][:].rearrange("p (c i) t -> p c t i", i=4),
                result[:, :, g * P : (g + 1) * P].rearrange("p t (c i) -> p c t i", i=4),
            )
        for g in (1, 0):
            cols = slice(g * P, (g + 1) * P)
            nc.vector.quantize_mx(
                result_codes[:, cols].bitcast(FP8X4),
                result_scales[:, cols],
                rounded[g][:].rearrange("p m t -> p (m t)"),
            )
        nc.sync.dma_start(out_1[0].rearrange("p c r -> p (c r)").bitcast(I32), result_codes[:].bitcast(I32))
        for quad in range(4):
            queue = nc.scalar if quad % 2 else nc.sync
            queue.dma_start(
                out_2[0, 4 * quad : 4 * quad + 4, :].bitcast(I32),
                result_scales[32 * quad : 32 * quad + 4, :].bitcast(I32),
            )
